import numpy as np
import ml_dtypes


def mxq(x, axis, fmt="e4m3"):
    dtype, down = {"e4m3": (ml_dtypes.float8_e4m3fn, 7), "e5m2": (ml_dtypes.float8_e5m2, 14)}[fmt]
    v = np.moveaxis(np.asarray(x, np.float32).astype(ml_dtypes.bfloat16).astype(np.float64), axis, -1)
    blocks = v.reshape(v.shape[:-1] + (-1, 32))
    amax = np.abs(blocks).max(-1, keepdims=True)
    byte = np.maximum(np.where(amax > 0, np.frexp(amax)[1] - 1 + 127, 0) - down, 1)
    scale = np.exp2(byte - 127.0)
    codes = (blocks / scale).astype(np.float32).astype(dtype).astype(np.float64)
    return np.moveaxis((codes * scale).reshape(v.shape), -1, axis)


WIDE = False


def mx_kscale(k):
    if not WIDE:
        return np.ones(k)
    levels = np.array([10, -10, 5, -5, 0])
    if k % 512:
        return np.exp2(np.random.permutation(np.resize(levels, k // 32))).repeat(32)
    a = np.empty((k // 512, 16))
    for p in range(k // 512):
        a[p, :8] = np.random.permutation(np.resize(levels, 8))
        for g in range(8):
            far = levels[np.abs(levels - a[p, g]) >= 10]
            a[p, g + 8] = far[np.random.randint(len(far))]
    return np.exp2(a.ravel()).repeat(32)


BF16 = ml_dtypes.bfloat16


def bf(x):
    return np.asarray(x, np.float32).astype(BF16)


def f64(x):
    return np.asarray(x).astype(np.float64)

E4M3FN = np.array([(-1.0 if i & 128 else 1.0) * ((1.0 + (i & 7) / 8.0) * 2.0 ** (((i >> 3) & 15) - 7) if i & 120 else (i & 7) * 2.0 ** -9) for i in range(256)])


def e4m3fn_bytes(y):
    return np.clip(np.asarray(y, np.float64), -448.0, 448.0).astype(np.float32).astype(ml_dtypes.float8_e4m3fn).view(np.uint8)


def e4m3fn_values(b):
    return E4M3FN[b]

def planes(Y):
    n, m = Y.shape
    b = f64(bf(Y)).reshape(n // 32, 32, m)
    amax = np.abs(b).max(1)
    byte = np.clip(np.where(amax > 0, np.frexp(amax)[1] - 1 + 127 - 7, 1), 1, 254)
    codes = (b * np.exp2(127.0 - byte)[:, None, :]).reshape(n, m).astype(np.float32).astype(ml_dtypes.float8_e4m3fn).view(np.uint8)
    words = codes.reshape(n // 512, 128, 4, m).transpose(0, 1, 3, 2)
    return np.ascontiguousarray(words), np.ascontiguousarray(byte.astype(np.uint8).reshape(n // 512, 16, m))


B, R, K, C, F = 512, 4, 2048, 1024, 1024

def setup_inputs():
    s = mx_kscale(K)
    r = mx_kscale(C)
    feats = (np.random.randn(B, K) + 0.7 * np.random.randn(1, K)) * np.exp(0.3 * np.random.randn(1, K)) * s
    X_mean = bf(feats.mean(axis=0, keepdims=True))
    centred = feats - f64(X_mean)
    X_scale = (np.abs(centred).max(axis=0, keepdims=True) / 448.0).astype(np.float32)
    X_bytes = e4m3fn_bytes(centred / f64(X_scale))
    U = bf(np.random.randn(K, F) / np.sqrt(K) / s[:, None])
    T = bf(np.random.randn(B * R, C) * r)
    V = bf(np.random.randn(C, F) / np.sqrt(C) / r[:, None])
    b_img = bf(0.3 * np.random.randn(1, F))
    b_txt = bf(0.3 * np.random.randn(1, F))
    gain = bf(np.exp(0.8 * np.random.randn(1, F)))
    return {"X_bytes": X_bytes, "X_scale": X_scale, "X_mean": X_mean, "U": U, "T": T, "V": V,
            "b_img": b_img, "b_txt": b_txt, "gain": gain}

def reference(X_bytes, X_scale, X_mean, U, T, V, b_img, b_txt, gain):
    X = e4m3fn_values(X_bytes) * np.repeat(f64(X_scale), B, axis=0) + f64(X_mean)
    A = (mxq(X, 1, "e4m3") @ mxq(f64(U), 0, "e4m3")) + f64(b_img)
    H = (mxq(f64(T), 1, "e4m3") @ mxq(f64(V), 0, "e4m3")) + f64(b_txt)
    joint = np.tanh(A.reshape(B, 1, F) * H.reshape(B, R, F))
    y = joint * f64(gain).reshape(1, 1, F)
    Y = y.reshape(B * R, F).T
    words, scales = planes(Y)
    return y, words, scales

@@ -1,0 +1,450 @@
+from contextlib import ExitStack
+
+import concourse.mybir as mybir
+from concourse.masks import make_identity
+
+B, R, K, C, F = 512, 4, 2048, 1024, 1024
+FLOPS = 2 * B * K * F + 2 * B * R * C * F
+
+F32 = mybir.dt.float32
+BF16 = mybir.dt.bfloat16
+U32 = mybir.dt.uint32
+I32 = mybir.dt.int32
+U8 = mybir.dt.uint8
+FP8 = mybir.dt.float8_e4m3fn
+FP8X4 = mybir.dt.float8_e4m3fn_x4
+ACT = mybir.ActivationFunctionType
+ALU = mybir.AluOpType
+
+P = 128
+PACK = 4
+SPAN = P * PACK
+X_PASSES = K // SPAN
+T_PASSES = C // SPAN
+HALVES = F // SPAN
+GROUPS = B * R // SPAN
+UNIT_ORDER = [(0, 0), (0, 1), (1, 0), (1, 1)] + [(g, b) for b in range(2, GROUPS) for g in range(HALVES)]
+UNITS = len(UNIT_ORDER)
+POOL_TOKENS = 0
+
+
+def tile_vqa_hadamard_fusion_b15_kernel(
+    tc, X_bytes, X_scale, X_mean, U, T, V, b_img, b_txt, gain, out_0, out_1, out_2
+):
+    nc = tc.nc
+    y_rows = out_0.rearrange("i j f -> (i j) f")
+    words_out = out_1.rearrange("g p m t -> g p (m t)").bitcast(I32)
+    scales_out = out_2.bitcast(I32)
+
+    with ExitStack() as ctx:
+        sb = ctx.enter_context(tc.tile_pool(name="sb", bufs=1))
+        psum = ctx.enter_context(tc.psum_pool(name="psum", bufs=1))
+        ctx.enter_context(tc.manual_schedule())
+
+        def bank(i):
+            return psum.tile([P, SPAN], F32, name="bank%d" % i)
+
+        x_raw, x_wide, x_banks, x_planes, x_woven, x_mx = {}, {}, {}, {}, {}, {}
+        w_raw, w_woven, w_mx = {}, {}, {}
+        t_raw, t_banks, t_woven, t_mx = {}, {}, {}, {}
+        a_banks, h_banks, z, y_banks, y_stage, y_woven = {}, {}, {}, {}, {}, {}
+
+        def quantize(src, tag, bufs):
+            codes = sb.tile([P, SPAN], U32, name=tag + "_codes", bufs=bufs, align_bytes=64)
+            scales = sb.tile([P, SPAN], U8, name=tag + "_scales", bufs=bufs, align_bytes=64)
+            nc.vector.quantize_mx(out=codes[:].bitcast(FP8X4), scales=scales[:], in_=src)
+            return codes, scales
+
+        def mx_pass(acc, weights, t, moving, first, last):
+            cols = slice(P * t, P * (t + 1))
+            nc.tensor.matmul_mx(
+                out=acc[:],
+                lhsT=weights[0][:, cols].bitcast(FP8X4),
+                lhsT_scale=weights[1][:, cols],
+                rhs=moving[0][:].bitcast(FP8X4),
+                rhs_scale=moving[1][:],
+                start=first,
+                stop=last,
+            )
+
+        def copy_on(engine, out, in_):
+            if engine == "scalar":
+                nc.scalar.copy(out=out, in_=in_)
+            else:
+                nc.vector.tensor_copy(out=out, in_=in_)
+
+        def load_x(c):
+            x_raw[c] = sb.tile([P, GROUPS, SPAN], U8, name="x_bytes", bufs=X_PASSES)
+            nc.sync.dma_start(
+                out=x_raw[c][:], in_=X_bytes[:, SPAN * c : SPAN * (c + 1)].rearrange("(b p) k -> p b k", p=P)
+            )
+
+        def load_channels(vec, name, dtype, queue):
+            n = vec.shape[1] // SPAN
+            vals = sb.tile([P, n, PACK], dtype, name=name)
+            queue.dma_start(out=vals[:], in_=vec.rearrange("o (g p t) -> p (o g) t", p=P, t=PACK))
+            return vals
+
+        def load_w(which, c, g):
+            W = U if which == "u" else V
+            raw = sb.tile([P, PACK, SPAN], BF16, name="w_raw", bufs=8)
+            w_raw[which, c, g] = raw
+            nc.sync.dma_start(
+                out=raw[:],
+                in_=W[SPAN * c : SPAN * (c + 1), SPAN * g : SPAN * (g + 1)].rearrange("(p j) f -> p j f", j=PACK),
+            )
+
+        def load_t(b):
+            t_raw[b] = sb.tile([P, PACK, C], BF16, name="t_raw", bufs=2)
+            nc.sync.dma_start(
+                out=t_raw[b][:], in_=T[SPAN * b : SPAN * (b + 1), :].rearrange("(s p) k -> p s k", p=P)
+            )
+
+        def widen_x(c, b0, b1, engine):
+            if c not in x_wide:
+                x_wide[c] = sb.tile([P, GROUPS * SPAN], BF16, name="x_wide", tag="bf16_rows", bufs=4, align_bytes=64)
+            src = x_raw[c][:, b0:b1, :].rearrange("p b k -> p (b k)").bitcast(FP8)
+            dst = x_wide[c][:, SPAN * b0 : SPAN * b1]
+            if engine == "scalar":
+                nc.scalar.activation(out=dst, in_=src, func=ACT.Copy)
+            else:
+                nc.vector.tensor_copy(out=dst, in_=src)
+
+        def turn_x(c):
+            words = x_wide[c][:].bitcast(F32)
+            for u in range(2):
+                x_banks[c, u] = bank(4 + 2 * (c % 2) + u)
+                for b in range(GROUPS):
+                    nc.tensor.transpose(
+                        x_banks[c, u][:, P * b : P * (b + 1)], words[:, 256 * b + u : 256 * (b + 1) : 2], ident[:]
+                    )
+
+        def scale_x(c):
+            x_planes[c] = sb.tile([P, PACK, SPAN], BF16, name="x_planes", bufs=3)
+            for t in range(PACK):
+                u, e = divmod(t, 2)
+                nc.scalar.activation(
+                    out=x_planes[c][:, t, :],
+                    in_=x_banks[c, u][:].bitcast(BF16)[:, e::2],
+                    func=ACT.Identity,
+                    scale=x_scale[:, c, t : t + 1],
+                    bias=x_mean[:, c, t : t + 1],
+                )
+
+        def interleave(engine, dst, src):
+            copy_on(
+                engine,
+                dst.rearrange("p (c i t) -> p c t i", i=4, t=PACK),
+                src.rearrange("p t (c i) -> p c t i", i=4),
+            )
+
+        def weave_x(c):
+            x_woven[c] = sb.tile([P, PACK * SPAN], BF16, name="x_woven", tag="woven", bufs=4, align_bytes=64)
+            interleave("vector", x_woven[c][:], x_planes[c][:])
+
+        def quant_x(c):
+            x_mx[c] = quantize(x_woven[c][:], "x", X_PASSES)
+
+        def weave_w(which, c, g, engine):
+            dst = sb.tile([P, PACK * SPAN], BF16, name="w_woven", tag="woven", bufs=4, align_bytes=64)
+            w_woven[which, c, g] = dst
+            copy_on(
+                engine,
+                dst[:].rearrange("p (t a l j) -> p a t l j", t=PACK, l=2, j=PACK),
+                w_raw[which, c, g][:].rearrange("p j (a l t) -> p a t l j", l=2, t=PACK),
+            )
+
+        def quant_w(which, c, g):
+            w_mx[which, c, g] = quantize(w_woven[which, c, g][:], which, 4)
+
+        def turn_t(b, bank0):
+            words = t_raw[b][:].bitcast(F32)
+            for s in range(PACK):
+                t_banks[b, s] = bank(bank0 + s)
+                for c in range(T_PASSES):
+                    for u in range(2):
+                        o = P * (2 * c + u)
+                        nc.tensor.transpose(
+                            t_banks[b, s][:, o : o + P], words[:, s, 256 * c + u : 256 * (c + 1) : 2], ident[:]
+                        )
+
+        def weave_t(b):
+            t_woven[b] = sb.tile([P, T_PASSES, PACK * SPAN], BF16, name="t_woven", bufs=2, align_bytes=64)
+            words = t_woven[b][:].bitcast(F32)
+            for s in range(PACK):
+                nc.scalar.copy(
+                    out=words[:, :, 256 * s : 256 * (s + 1)].rearrange("p c (r u) -> p c r u", u=2),
+                    in_=t_banks[b, s][:].rearrange("p (c u r) -> p c r u", c=T_PASSES, u=2),
+                )
+
+        def quant_t(b, c):
+            t_mx[b, c] = quantize(t_woven[b][:, c, :], "t", GROUPS * T_PASSES)
+
+        def a_pass(g, c, t, bank0):
+            if c == 0:
+                a_banks[g, t] = bank(bank0 + t)
+            mx_pass(a_banks[g, t], w_mx["u", c, g], t, x_mx[c], c == 0, c == X_PASSES - 1)
+
+        def a_out(g, t):
+            nc.scalar.activation(
+                out=a_sb[:, g, t, :], in_=a_banks[g, t][:], func=ACT.Identity, bias=bias_img[:, g, t : t + 1]
+            )
+
+        def h_mm(n, t):
+            g, b = UNIT_ORDER[n]
+            h_banks[n, t] = bank(4 + t)
+            for c in range(T_PASSES):
+                mx_pass(h_banks[n, t], w_mx["v", c, g], t, t_mx[b, c], c == 0, c == T_PASSES - 1)
+
+        def product(n, t):
+            g, b = UNIT_ORDER[n]
+            if t == 0:
+                z[n] = sb.tile([P, PACK, SPAN], F32, name="z", bufs=3)
+            nc.vector.scalar_tensor_tensor(
+                out=z[n][:, t, :].rearrange("p (i j) -> p i j", j=R),
+                in0=h_banks[n, t][:].rearrange("p (i j) -> p i j", j=R),
+                scalar=bias_txt[:, g, t : t + 1],
+                in1=a_sb[:, g, t, P * b : P * (b + 1)].unsqueeze(2).to_broadcast([P, P, R]),
+                op0=ALU.add,
+                op1=ALU.mult,
+            )
+
+        def squash(n, t0, t1):
+            nc.scalar.activation(out=z[n][:, t0:t1, :], in_=z[n][:, t0:t1, :], func=ACT.Tanh)
+
+        def apply_gain(n, t, engine):
+            g = UNIT_ORDER[n][0]
+            if engine == "scalar":
+                nc.scalar.activation(out=z[n][:, t, :], in_=z[n][:, t, :], func=ACT.Copy, scale=gain_f[:, g, t : t + 1])
+            else:
+                nc.vector.tensor_scalar(
+                    out=z[n][:, t, :], in0=z[n][:, t, :], scalar1=gain_f[:, g, t : t + 1], scalar2=None, op0=ALU.mult
+                )
+
+        def turn_y(n, s0, s1):
+            for s in range(s0, s1):
+                y_banks[n, s] = bank(s)
+                for t in range(PACK):
+                    nc.tensor.transpose(y_banks[n, s][:, P * t : P * (t + 1)], z[n][:, t, P * s : P * (s + 1)], ident[:])
+
+        def y_out(n, s, engine):
+            if s == 0:
+                y_stage[n] = sb.tile([P, PACK, SPAN], F32, name="y_stage", bufs=2)
+            copy_on(
+                engine,
+                y_stage[n][:, s, :].rearrange("m (p t) -> m p t", t=PACK),
+                y_banks[n, s][:].rearrange("m (t p) -> m p t", t=PACK),
+            )
+
+        def store_y(n, s0, s1):
+            g, b = UNIT_ORDER[n]
+            rows = y_rows[SPAN * b + P * s0 : SPAN * b + P * s1, SPAN * g : SPAN * (g + 1)]
+            nc.sync.dma_start(out=rows.rearrange("(s m) f -> m s f", m=P), in_=y_stage[n][:, s0:s1, :])
+
+        def weave_y_pool(n, m1):
+            y_woven[n] = sb.tile([P, PACK * SPAN], BF16, name="y_woven", tag="bf16_rows", bufs=4, align_bytes=64)
+            if m1 > 0:
+                nc.gpsimd.tensor_scalar(
+                    out=y_woven[n][:, : PACK * m1].rearrange("p (m t) -> p m t", t=PACK),
+                    in0=z[n][:, :, :m1].rearrange("p t m -> p m t"),
+                    scalar1=1.0,
+                    scalar2=1.0,
+                    op0=ALU.mult,
+                    op1=ALU.mult,
+                )
+
+        def weave_y(n, m0):
+            interleave("vector", y_woven[n][:, PACK * m0 :], z[n][:, :, m0:])
+
+        def quant_y(n):
+            g, b = UNIT_ORDER[n]
+            codes = sb.tile([P, SPAN], U32, name="y_codes", bufs=3, align_bytes=64)
+            nc.vector.quantize_mx(
+                out=codes[:].bitcast(FP8X4), scales=y_scales[4 * g :, SPAN * b : SPAN * (b + 1)], in_=y_woven[n][:]
+            )
+            nc.sync.dma_start(out=words_out[g, :, SPAN * b : SPAN * (b + 1)], in_=codes[:].bitcast(I32))
+
+        def store_scales(b0, b1):
+            cols = slice(P * b0, P * b1)
+            for q in range(4):
+                nc.sync.dma_start(
+                    out=scales_out[:, 4 * q : 4 * q + 4, cols], in_=y_scales[32 * q : 32 * q + 8, :].bitcast(I32)[:, cols]
+                )
+
+        ident = sb.tile([P, P], F32, name="ident")
+        make_identity(nc, ident[:])
+        a_sb = sb.tile([P, HALVES, PACK, SPAN], F32, name="a_sb")
+
+        y_scales = sb.tile([P, GROUPS * SPAN], U8, name="y_scales", align_bytes=64)
+        load_x(0)
+        x_scale = load_channels(X_scale, "x_scale", F32, nc.scalar)
+        x_mean = load_channels(X_mean, "x_mean", BF16, nc.scalar)
+        load_x(1)
+        load_x(2)
+        load_x(3)
+        load_w("u", 0, 0)
+        load_w("u", 1, 0)
+        load_t(0)
+        load_w("u", 2, 0)
+        load_w("u", 3, 0)
+        load_w("v", 0, 0)
+        load_w("v", 1, 0)
+        bias_img = load_channels(b_img, "bias_img", BF16, nc.sync)
+        bias_txt = load_channels(b_txt, "bias_txt", BF16, nc.sync)
+        gain_bf = load_channels(gain, "gain_bf", BF16, nc.sync)
+        load_w("u", 0, 1)
+        load_w("v", 0, 1)
+        load_t(1)
+
+        widen_x(0, 0, 2, "vector")
+        widen_x(0, 2, 4, "vector")
+        widen_x(1, 0, 2, "scalar")
+        widen_x(1, 2, 4, "vector")
+        turn_x(0)
+        turn_x(1)
+        widen_x(2, 0, 4, "vector")
+        widen_x(3, 0, 4, "vector")
+        scale_x(0)
+        turn_x(2)
+        weave_w("u", 0, 0, "vector")
+        load_w("u", 1, 1)
+        weave_x(0)
+        quant_w("u", 0, 0)
+        scale_x(1)
+        turn_x(3)
+        turn_t(0, 0)
+        load_t(2)
+        weave_w("u", 1, 0, "vector")
+        load_w("u", 2, 1)
+        quant_x(0)
+        weave_x(1)
+        quant_w("u", 1, 0)
+        scale_x(2)
+        weave_w("u", 2, 0, "vector")
+        load_w("u", 3, 1)
+        quant_x(1)
+        weave_x(2)
+        quant_w("u", 2, 0)
+        scale_x(3)
+        weave_t(0)
+        weave_w("u", 3, 0, "scalar")
+        load_w("v", 1, 1)
+        weave_x(3)
+        quant_x(2)
+        for c in range(3):
+            for t in range(PACK):
+                a_pass(0, c, t, 0)
+        weave_w("v", 0, 0, "vector")
+        quant_x(3)
+        quant_w("u", 3, 0)
+        for t in range(PACK):
+            a_pass(0, 3, t, 0)
+        quant_t(0, 0)
+        quant_w("v", 0, 0)
+        weave_w("v", 1, 0, "scalar")
+        quant_t(0, 1)
+        quant_w("v", 1, 0)
+        weave_w("u", 0, 1, "vector")
+        gain_f = sb.tile([P, HALVES, PACK], F32, name="gain_f")
+        nc.scalar.copy(out=gain_f[:], in_=gain_bf[:])
+        for t in range(PACK):
+            a_out(0, t)
+        for t in range(PACK):
+            h_mm(0, t)
+        weave_w("v", 0, 1, "scalar")
+
+        LAST = UNITS - 1
+        for n in range(UNITS + 1):
+            cur, nxt, prev, old = n < UNITS, n + 1 < UNITS, n >= 1, n >= 2
+            t_next = {2: 2, 4: 3}.get(n)
+            s_gain = n in (3, 5, 6, 7) and POOL_TOKENS == 0
+            pool = POOL_TOKENS if cur else 0
+            if s_gain:
+                apply_gain(n - 1, 0, "scalar")
+            if old:
+                for s in range(PACK):
+                    y_out(n - 2, s, "scalar")
+                    if s % 2 == 1:
+                        store_y(n - 2, s - 1, s + 1)
+            if n == 0:
+                turn_t(1, 0)
+                load_t(3)
+                weave_t(1)
+            if t_next:
+                turn_t(t_next, 0)
+                weave_t(t_next)
+            if n in (3, 5):
+                quant_t((n + 1) // 2, 0)
+                quant_t((n + 1) // 2, 1)
+            if prev:
+                for t in range(1 if s_gain else 0, PACK):
+                    if old and t == 2:
+                        quant_y(n - 2)
+                        if n - 2 == UNITS - 3:
+                            store_scales(0, GROUPS - 1)
+                    apply_gain(n - 1, t, "vector")
+                weave_y_pool(n - 1, pool)
+            if old and not t_next:
+                turn_y(n - 1, 0, 2)
+            if cur:
+                product(n, 0)
+                product(n, 1)
+            if n == 1:
+                weave_w("v", 1, 1, "scalar")
+            if cur:
+                squash(n, 0, 2)
+            if nxt and old:
+                h_mm(n + 1, 0)
+                h_mm(n + 1, 1)
+            if old:
+                if t_next:
+                    turn_y(n - 1, 0, 2)
+                else:
+                    turn_y(n - 1, 2, 4)
+            if cur:
+                product(n, 2)
+                squash(n, 2, 3)
+                product(n, 3)
+                squash(n, 3, 4)
+            if nxt and old:
+                h_mm(n + 1, 2)
+                h_mm(n + 1, 3)
+            if t_next:
+                turn_y(n - 1, 2, 4)
+            if n == 0:
+                quant_w("u", 0, 1)
+                weave_w("u", 1, 1, "vector")
+                quant_w("v", 0, 1)
+                quant_t(1, 0)
+                quant_t(1, 1)
+                for t in range(PACK):
+                    a_pass(1, 0, t, 0)
+                for t in range(PACK):
+                    h_mm(1, t)
+                weave_w("u", 2, 1, "vector")
+                weave_w("u", 3, 1, "scalar")
+                quant_w("u", 1, 1)
+                quant_w("u", 2, 1)
+                for c in (1, 2):
+                    for t in range(PACK):
+                        a_pass(1, c, t, 0)
+            if n == 1:
+                quant_w("u", 3, 1)
+                quant_w("v", 1, 1)
+                for t in range(PACK):
+                    a_pass(1, 3, t, 0)
+                    a_out(1, t)
+                for t in range(PACK):
+                    h_mm(2, t)
+                turn_y(0, 0, 4)
+            if prev and n < UNITS:
+                weave_y(n - 1, pool)
+        weave_y(LAST, 0)
+        for s in range(PACK - 1):
+            y_out(LAST, s, "scalar")
+            if s == 1:
+                store_y(LAST, 0, 2)
+        y_out(LAST, PACK - 1, "vector")
+        store_y(LAST, 2, PACK)
+        quant_y(LAST)
+        store_scales(GROUPS - 1, GROUPS)

@@ -25,7 +25,8 @@ HALVES = F // SPAN
 GROUPS = B * R // SPAN
 UNIT_ORDER = [(0, 0), (0, 1), (1, 0), (1, 1)] + [(g, b) for b in range(2, GROUPS) for g in range(HALVES)]
 UNITS = len(UNIT_ORDER)
-POOL_TOKENS = 0
+POOL_TOKENS = 256
+POOL_TOKENS_LONG = 448
 
 
 def tile_vqa_hadamard_fusion_b15_kernel(
@@ -139,14 +140,14 @@ def tile_vqa_hadamard_fusion_b15_kernel(
             )
 
         def weave_x(c):
-            x_woven[c] = sb.tile([P, PACK * SPAN], BF16, name="x_woven", tag="woven", bufs=4, align_bytes=64)
+            x_woven[c] = sb.tile([P, PACK * SPAN], BF16, name="x_woven", tag="woven", bufs=5, align_bytes=64)
             interleave("vector", x_woven[c][:], x_planes[c][:])
 
         def quant_x(c):
             x_mx[c] = quantize(x_woven[c][:], "x", X_PASSES)
 
         def weave_w(which, c, g, engine):
-            dst = sb.tile([P, PACK * SPAN], BF16, name="w_woven", tag="woven", bufs=4, align_bytes=64)
+            dst = sb.tile([P, PACK * SPAN], BF16, name="w_woven", tag="woven", bufs=5, align_bytes=64)
             w_woven[which, c, g] = dst
             copy_on(
                 engine,
@@ -190,11 +191,15 @@ def tile_vqa_hadamard_fusion_b15_kernel(
                 out=a_sb[:, g, t, :], in_=a_banks[g, t][:], func=ACT.Identity, bias=bias_img[:, g, t : t + 1]
             )
 
-        def h_mm(n, t):
+        def h_pass(n, t, c):
             g, b = UNIT_ORDER[n]
-            h_banks[n, t] = bank(4 + t)
+            if c == 0:
+                h_banks[n, t] = bank(4 + t)
+            mx_pass(h_banks[n, t], w_mx["v", c, g], t, t_mx[b, c], c == 0, c == T_PASSES - 1)
+
+        def h_mm(n, t):
             for c in range(T_PASSES):
-                mx_pass(h_banks[n, t], w_mx["v", c, g], t, t_mx[b, c], c == 0, c == T_PASSES - 1)
+                h_pass(n, t, c)
 
         def product(n, t):
             g, b = UNIT_ORDER[n]
@@ -212,14 +217,10 @@ def tile_vqa_hadamard_fusion_b15_kernel(
         def squash(n, t0, t1):
             nc.scalar.activation(out=z[n][:, t0:t1, :], in_=z[n][:, t0:t1, :], func=ACT.Tanh)
 
-        def apply_gain(n, t, engine):
+        def apply_gain(n, t, m0, m1):
             g = UNIT_ORDER[n][0]
-            if engine == "scalar":
-                nc.scalar.activation(out=z[n][:, t, :], in_=z[n][:, t, :], func=ACT.Copy, scale=gain_f[:, g, t : t + 1])
-            else:
-                nc.vector.tensor_scalar(
-                    out=z[n][:, t, :], in0=z[n][:, t, :], scalar1=gain_f[:, g, t : t + 1], scalar2=None, op0=ALU.mult
-                )
+            rows = z[n][:, t, m0:m1]
+            nc.vector.tensor_scalar(out=rows, in0=rows, scalar1=gain_bf[:, g, t : t + 1], scalar2=None, op0=ALU.mult)
 
         def turn_y(n, s0, s1):
             for s in range(s0, s1):
@@ -228,7 +229,7 @@ def tile_vqa_hadamard_fusion_b15_kernel(
                     nc.tensor.transpose(y_banks[n, s][:, P * t : P * (t + 1)], z[n][:, t, P * s : P * (s + 1)], ident[:])
 
         def y_out(n, s, engine):
-            if s == 0:
+            if n not in y_stage:
                 y_stage[n] = sb.tile([P, PACK, SPAN], F32, name="y_stage", bufs=2)
             copy_on(
                 engine,
@@ -241,20 +242,21 @@ def tile_vqa_hadamard_fusion_b15_kernel(
             rows = y_rows[SPAN * b + P * s0 : SPAN * b + P * s1, SPAN * g : SPAN * (g + 1)]
             nc.sync.dma_start(out=rows.rearrange("(s m) f -> m s f", m=P), in_=y_stage[n][:, s0:s1, :])
 
-        def weave_y_pool(n, m1):
-            y_woven[n] = sb.tile([P, PACK * SPAN], BF16, name="y_woven", tag="bf16_rows", bufs=4, align_bytes=64)
-            if m1 > 0:
+        def weave_y(n, m0, m1, engine):
+            if n not in y_woven:
+                y_woven[n] = sb.tile([P, PACK * SPAN], BF16, name="y_woven", tag="bf16_rows", bufs=4, align_bytes=64)
+            dst, src = y_woven[n][:, PACK * m0 : PACK * m1], z[n][:, :, m0:m1]
+            if engine == "gpsimd":
                 nc.gpsimd.tensor_scalar(
-                    out=y_woven[n][:, : PACK * m1].rearrange("p (m t) -> p m t", t=PACK),
-                    in0=z[n][:, :, :m1].rearrange("p t m -> p m t"),
+                    out=dst.rearrange("p (m t) -> p m t", t=PACK),
+                    in0=src.rearrange("p t m -> p m t"),
                     scalar1=1.0,
                     scalar2=1.0,
                     op0=ALU.mult,
                     op1=ALU.mult,
                 )
-
-        def weave_y(n, m0):
-            interleave("vector", y_woven[n][:, PACK * m0 :], z[n][:, :, m0:])
+            else:
+                interleave(engine, dst, src)
 
         def quant_y(n):
             g, b = UNIT_ORDER[n]
@@ -293,7 +295,7 @@ def tile_vqa_hadamard_fusion_b15_kernel(
         bias_txt = load_channels(b_txt, "bias_txt", BF16, nc.sync)
         gain_bf = load_channels(gain, "gain_bf", BF16, nc.sync)
         load_w("u", 0, 1)
-        load_w("v", 0, 1)
+        load_w("u", 1, 1)
         load_t(1)
 
         widen_x(0, 0, 2, "vector")
@@ -307,7 +309,7 @@ def tile_vqa_hadamard_fusion_b15_kernel(
         scale_x(0)
         turn_x(2)
         weave_w("u", 0, 0, "vector")
-        load_w("u", 1, 1)
+        load_w("u", 3, 1)
         weave_x(0)
         quant_w("u", 0, 0)
         scale_x(1)
@@ -321,130 +323,151 @@ def tile_vqa_hadamard_fusion_b15_kernel(
         quant_w("u", 1, 0)
         scale_x(2)
         weave_w("u", 2, 0, "vector")
-        load_w("u", 3, 1)
+        load_w("v", 1, 1)
         quant_x(1)
         weave_x(2)
         quant_w("u", 2, 0)
         scale_x(3)
         weave_t(0)
         weave_w("u", 3, 0, "scalar")
-        load_w("v", 1, 1)
+        load_w("v", 0, 1)
         weave_x(3)
         quant_x(2)
         for c in range(3):
             for t in range(PACK):
                 a_pass(0, c, t, 0)
-        weave_w("v", 0, 0, "vector")
+        weave_w("v", 0, 0, "scalar")
         quant_x(3)
         quant_w("u", 3, 0)
         for t in range(PACK):
             a_pass(0, 3, t, 0)
         quant_t(0, 0)
-        quant_w("v", 0, 0)
         weave_w("v", 1, 0, "scalar")
         quant_t(0, 1)
-        quant_w("v", 1, 0)
+        quant_w("v", 0, 0)
         weave_w("u", 0, 1, "vector")
-        gain_f = sb.tile([P, HALVES, PACK], F32, name="gain_f")
-        nc.scalar.copy(out=gain_f[:], in_=gain_bf[:])
+        quant_w("v", 1, 0)
         for t in range(PACK):
             a_out(0, t)
         for t in range(PACK):
             h_mm(0, t)
-        weave_w("v", 0, 1, "scalar")
+        weave_w("u", 1, 1, "vector")
 
         LAST = UNITS - 1
-        for n in range(UNITS + 1):
-            cur, nxt, prev, old = n < UNITS, n + 1 < UNITS, n >= 1, n >= 2
-            t_next = {2: 2, 4: 3}.get(n)
-            s_gain = n in (3, 5, 6, 7) and POOL_TOKENS == 0
-            pool = POOL_TOKENS if cur else 0
-            if s_gain:
-                apply_gain(n - 1, 0, "scalar")
-            if old:
-                for s in range(PACK):
-                    y_out(n - 2, s, "scalar")
-                    if s % 2 == 1:
-                        store_y(n - 2, s - 1, s + 1)
-            if n == 0:
-                turn_t(1, 0)
-                load_t(3)
-                weave_t(1)
-            if t_next:
-                turn_t(t_next, 0)
-                weave_t(t_next)
+
+        def gains(n):
+            for t in range(PACK):
+                if t == 2:
+                    quant_y(n - 1)
+                    if n - 1 == UNITS - 3:
+                        store_scales(0, GROUPS - 1)
+                apply_gain(n, t, 0, SPAN)
+
+        def y_pair_out(n, s0, engine0, engine1):
+            y_out(n, s0, engine0)
+            y_out(n, s0 + 1, engine1)
+            store_y(n, s0, s0 + 2)
+
+        def quant_t_both(b):
+            for c in range(T_PASSES):
+                quant_t(b, c)
+
+        turn_t(1, 0)
+        load_t(3)
+        weave_w("u", 3, 1, "scalar")
+        weave_t(1)
+        for t in range(PACK):
+            product(0, t)
+        squash(0, 0, 2)
+        squash(0, 2, 4)
+        quant_w("u", 0, 1)
+        quant_w("u", 1, 1)
+        for t in range(PACK):
+            for c in range(2):
+                a_pass(1, c, t, 0)
+        weave_w("u", 2, 1, "vector")
+        quant_w("u", 3, 1)
+        quant_t_both(1)
+        for t in range(PACK):
+            h_mm(1, t)
+        weave_w("v", 1, 1, "scalar")
+        quant_w("u", 2, 1)
+        weave_w("v", 0, 1, "vector")
+        for t in range(PACK):
+            for c in range(2, X_PASSES):
+                a_pass(1, c, t, 0)
+            a_out(1, t)
+
+        apply_gain(0, 0, 0, SPAN)
+        apply_gain(0, 1, 0, SPAN)
+        quant_w("v", 0, 1)
+        apply_gain(0, 2, 0, SPAN)
+        apply_gain(0, 3, 0, SPAN)
+        weave_y(0, 0, POOL_TOKENS, "gpsimd")
+        for t in range(PACK):
+            product(1, t)
+            h_pass(2, t, 0)
+        squash(1, 0, 2)
+        squash(1, 2, 4)
+        turn_y(0, 0, 2)
+        quant_w("v", 1, 1)
+        weave_y(0, POOL_TOKENS, SPAN, "vector")
+        for t in range(PACK):
+            h_pass(2, t, 1)
+        turn_y(0, 2, PACK)
+
+        for n in range(2, UNITS):
+            nxt = n < LAST
+            late = n in (2, 4)
+            if nxt:
+                y_pair_out(n - 2, 0, "vector" if late else "scalar", "scalar")
+                y_pair_out(n - 2, 2, "scalar", "scalar")
+            if late:
+                turn_t(n // 2 + 1, 0)
+                weave_t(n // 2 + 1)
             if n in (3, 5):
-                quant_t((n + 1) // 2, 0)
-                quant_t((n + 1) // 2, 1)
-            if prev:
-                for t in range(1 if s_gain else 0, PACK):
-                    if old and t == 2:
-                        quant_y(n - 2)
-                        if n - 2 == UNITS - 3:
-                            store_scales(0, GROUPS - 1)
-                    apply_gain(n - 1, t, "vector")
-                weave_y_pool(n - 1, pool)
-            if old and not t_next:
+                quant_t_both((n + 1) // 2)
+            gains(n - 1)
+            pool = POOL_TOKENS_LONG if n >= LAST - 1 else POOL_TOKENS
+            weave_y(n - 1, 0, pool, "gpsimd")
+            if not late:
                 turn_y(n - 1, 0, 2)
-            if cur:
-                product(n, 0)
-                product(n, 1)
-            if n == 1:
-                weave_w("v", 1, 1, "scalar")
-            if cur:
-                squash(n, 0, 2)
-            if nxt and old:
+            product(n, 0)
+            product(n, 1)
+            if n == LAST:
+                y_pair_out(n - 1, 0, "scalar", "scalar")
+            squash(n, 0, 2)
+            if nxt:
                 h_mm(n + 1, 0)
                 h_mm(n + 1, 1)
-            if old:
-                if t_next:
-                    turn_y(n - 1, 0, 2)
-                else:
-                    turn_y(n - 1, 2, 4)
-            if cur:
-                product(n, 2)
-                squash(n, 2, 3)
-                product(n, 3)
-                squash(n, 3, 4)
-            if nxt and old:
+            if late:
+                turn_y(n - 1, 0, 2)
+            else:
+                turn_y(n - 1, 2, 4)
+            product(n, 2)
+            squash(n, 2, 3)
+            product(n, 3)
+            squash(n, 3, 4)
+            if nxt:
                 h_mm(n + 1, 2)
                 h_mm(n + 1, 3)
-            if t_next:
+            if late:
                 turn_y(n - 1, 2, 4)
-            if n == 0:
-                quant_w("u", 0, 1)
-                weave_w("u", 1, 1, "vector")
-                quant_w("v", 0, 1)
-                quant_t(1, 0)
-                quant_t(1, 1)
-                for t in range(PACK):
-                    a_pass(1, 0, t, 0)
-                for t in range(PACK):
-                    h_mm(1, t)
-                weave_w("u", 2, 1, "vector")
-                weave_w("u", 3, 1, "scalar")
-                quant_w("u", 1, 1)
-                quant_w("u", 2, 1)
-                for c in (1, 2):
-                    for t in range(PACK):
-                        a_pass(1, c, t, 0)
-            if n == 1:
-                quant_w("u", 3, 1)
-                quant_w("v", 1, 1)
-                for t in range(PACK):
-                    a_pass(1, 3, t, 0)
-                    a_out(1, t)
-                for t in range(PACK):
-                    h_mm(2, t)
-                turn_y(0, 0, 4)
-            if prev and n < UNITS:
-                weave_y(n - 1, pool)
-        weave_y(LAST, 0)
-        for s in range(PACK - 1):
-            y_out(LAST, s, "scalar")
-            if s == 1:
-                store_y(LAST, 0, 2)
-        y_out(LAST, PACK - 1, "vector")
-        store_y(LAST, 2, PACK)
+            if n == LAST - 1:
+                y_pair_out(n - 1, 0, "vector", "vector")
+                y_pair_out(n - 1, 2, "scalar", "scalar")
+            elif n == LAST:
+                y_pair_out(n - 1, 2, "vector", "vector")
+            weave_y(n - 1, pool, SPAN, "vector")
+        for t in range(PACK):
+            apply_gain(LAST, t, 0, SPAN // 2)
+        turn_y(LAST, 0, 2)
+        for t in range(PACK):
+            apply_gain(LAST, t, SPAN // 2, SPAN)
+        turn_y(LAST, 2, PACK)
+        quant_y(LAST - 1)
+        weave_y(LAST, 0, SPAN, "vector")
+        y_pair_out(LAST, 0, "scalar", "scalar")
+        y_pair_out(LAST, 2, "scalar", "scalar")
         quant_y(LAST)
         store_scales(GROUPS - 1, GROUPS)

@@ -27,6 +27,11 @@ UNIT_ORDER = [(0, 0), (0, 1), (1, 0), (1, 1)] + [(g, b) for b in range(2, GROUPS
 UNITS = len(UNIT_ORDER)
 POOL_TOKENS = 256
 POOL_TOKENS_LONG = 448
+SCALAR_GAIN = (4, 5)
+TQ = {3: 2, 5: 3}
+T3_AT = 3
+VCOPY = 0
+SPREAD = 0
 
 
 def tile_vqa_hadamard_fusion_b15_kernel(
@@ -54,7 +59,7 @@ def tile_vqa_hadamard_fusion_b15_kernel(
             codes = sb.tile([P, SPAN], U32, name=tag + "_codes", bufs=bufs, align_bytes=64)
             scales = sb.tile([P, SPAN], U8, name=tag + "_scales", bufs=bufs, align_bytes=64)
             nc.vector.quantize_mx(out=codes[:].bitcast(FP8X4), scales=scales[:], in_=src)
-            return codes, scales
+            return codes[:], scales[:]
 
         def mx_pass(acc, weights, t, moving, first, last):
             cols = slice(P * t, P * (t + 1))
@@ -62,8 +67,8 @@ def tile_vqa_hadamard_fusion_b15_kernel(
                 out=acc[:],
                 lhsT=weights[0][:, cols].bitcast(FP8X4),
                 lhsT_scale=weights[1][:, cols],
-                rhs=moving[0][:].bitcast(FP8X4),
-                rhs_scale=moving[1][:],
+                rhs=moving[0].bitcast(FP8X4),
+                rhs_scale=moving[1],
                 start=first,
                 stop=last,
             )
@@ -74,10 +79,10 @@ def tile_vqa_hadamard_fusion_b15_kernel(
             else:
                 nc.vector.tensor_copy(out=out, in_=in_)
 
-        def load_x(c):
-            x_raw[c] = sb.tile([P, GROUPS, SPAN], U8, name="x_bytes", bufs=X_PASSES)
+        def load_x(h):
+            x_raw[h] = sb.tile([P, GROUPS, K // 2], U8, name="x_bytes", bufs=2)
             nc.sync.dma_start(
-                out=x_raw[c][:], in_=X_bytes[:, SPAN * c : SPAN * (c + 1)].rearrange("(b p) k -> p b k", p=P)
+                out=x_raw[h][:], in_=X_bytes[:, K // 2 * h : K // 2 * (h + 1)].rearrange("(b p) k -> p b k", p=P)
             )
 
         def load_channels(vec, name, dtype, queue):
@@ -101,24 +106,23 @@ def tile_vqa_hadamard_fusion_b15_kernel(
                 out=t_raw[b][:], in_=T[SPAN * b : SPAN * (b + 1), :].rearrange("(s p) k -> p s k", p=P)
             )
 
-        def widen_x(c, b0, b1, engine):
-            if c not in x_wide:
-                x_wide[c] = sb.tile([P, GROUPS * SPAN], BF16, name="x_wide", tag="bf16_rows", bufs=4, align_bytes=64)
-            src = x_raw[c][:, b0:b1, :].rearrange("p b k -> p (b k)").bitcast(FP8)
-            dst = x_wide[c][:, SPAN * b0 : SPAN * b1]
+        def widen_x(h, b0, b1, engine):
+            if h not in x_wide:
+                x_wide[h] = sb.tile([P, GROUPS * K // 2], BF16, name="x_wide", tag="turned_rows", bufs=2, align_bytes=64)
+            src = x_raw[h][:, b0:b1, :].rearrange("p b k -> p (b k)").bitcast(FP8)
+            dst = x_wide[h][:, K // 2 * b0 : K // 2 * b1]
             if engine == "scalar":
                 nc.scalar.activation(out=dst, in_=src, func=ACT.Copy)
             else:
                 nc.vector.tensor_copy(out=dst, in_=src)
 
         def turn_x(c):
-            words = x_wide[c][:].bitcast(F32)
+            words = x_wide[c // 2][:].bitcast(F32)
             for u in range(2):
                 x_banks[c, u] = bank(4 + 2 * (c % 2) + u)
                 for b in range(GROUPS):
-                    nc.tensor.transpose(
-                        x_banks[c, u][:, P * b : P * (b + 1)], words[:, 256 * b + u : 256 * (b + 1) : 2], ident[:]
-                    )
+                    w0 = 512 * b + 256 * (c % 2)
+                    nc.tensor.transpose(x_banks[c, u][:, P * b : P * (b + 1)], words[:, w0 + u : w0 + 256 : 2], ident[:])
 
         def scale_x(c):
             x_planes[c] = sb.tile([P, PACK, SPAN], BF16, name="x_planes", bufs=3)
@@ -151,16 +155,16 @@ def tile_vqa_hadamard_fusion_b15_kernel(
             w_woven[which, c, g] = dst
             copy_on(
                 engine,
-                dst[:].rearrange("p (t a l j) -> p a t l j", t=PACK, l=2, j=PACK),
-                w_raw[which, c, g][:].rearrange("p j (a l t) -> p a t l j", l=2, t=PACK),
+                dst[:].rearrange("p (t a l j) -> p a j l t", t=PACK, l=2, j=PACK),
+                w_raw[which, c, g][:].rearrange("p j (a l t) -> p a j l t", l=2, t=PACK),
             )
 
         def quant_w(which, c, g):
             w_mx[which, c, g] = quantize(w_woven[which, c, g][:], which, 4)
 
-        def turn_t(b, bank0):
+        def turn_t(b, bank0, s0, s1):
             words = t_raw[b][:].bitcast(F32)
-            for s in range(PACK):
+            for s in range(s0, s1):
                 t_banks[b, s] = bank(bank0 + s)
                 for c in range(T_PASSES):
                     for u in range(2):
@@ -169,17 +173,25 @@ def tile_vqa_hadamard_fusion_b15_kernel(
                             t_banks[b, s][:, o : o + P], words[:, s, 256 * c + u : 256 * (c + 1) : 2], ident[:]
                         )
 
-        def weave_t(b):
-            t_woven[b] = sb.tile([P, T_PASSES, PACK * SPAN], BF16, name="t_woven", bufs=2, align_bytes=64)
+        def weave_t(b, s0, s1):
+            if b not in t_woven:
+                t_woven[b] = sb.tile([P, T_PASSES, PACK * SPAN], BF16, name="t_woven", tag="turned_rows", bufs=2, align_bytes=64)
             words = t_woven[b][:].bitcast(F32)
-            for s in range(PACK):
+            for s in range(s0, s1):
                 nc.scalar.copy(
                     out=words[:, :, 256 * s : 256 * (s + 1)].rearrange("p c (r u) -> p c r u", u=2),
                     in_=t_banks[b, s][:].rearrange("p (c u r) -> p c r u", c=T_PASSES, u=2),
                 )
 
-        def quant_t(b, c):
-            t_mx[b, c] = quantize(t_woven[b][:, c, :], "t", GROUPS * T_PASSES)
+        def quant_t(b):
+            codes = sb.tile([P, T_PASSES * SPAN], U32, name="t_codes", bufs=GROUPS, align_bytes=64)
+            scales = sb.tile([P, T_PASSES * SPAN], U8, name="t_scales", bufs=GROUPS, align_bytes=64)
+            nc.vector.quantize_mx(
+                out=codes[:].bitcast(FP8X4), scales=scales[:], in_=t_woven[b][:].rearrange("p c w -> p (c w)")
+            )
+            for c in range(T_PASSES):
+                cols = slice(SPAN * c, SPAN * (c + 1))
+                t_mx[b, c] = codes[:, cols], scales[:, cols]
 
         def a_pass(g, c, t, bank0):
             if c == 0:
@@ -244,7 +256,7 @@ def tile_vqa_hadamard_fusion_b15_kernel(
 
         def weave_y(n, m0, m1, engine):
             if n not in y_woven:
-                y_woven[n] = sb.tile([P, PACK * SPAN], BF16, name="y_woven", tag="bf16_rows", bufs=4, align_bytes=64)
+                y_woven[n] = sb.tile([P, PACK * SPAN], BF16, name="y_woven", bufs=3, align_bytes=64)
             dst, src = y_woven[n][:, PACK * m0 : PACK * m1], z[n][:, :, m0:m1]
             if engine == "gpsimd":
                 nc.gpsimd.tensor_scalar(
@@ -279,16 +291,15 @@ def tile_vqa_hadamard_fusion_b15_kernel(
 
         y_scales = sb.tile([P, GROUPS * SPAN], U8, name="y_scales", align_bytes=64)
         load_x(0)
-        x_scale = load_channels(X_scale, "x_scale", F32, nc.scalar)
-        x_mean = load_channels(X_mean, "x_mean", BF16, nc.scalar)
         load_x(1)
-        load_x(2)
-        load_x(3)
+        x_scale = load_channels(X_scale, "x_scale", F32, nc.sync)
+        x_mean = load_channels(X_mean, "x_mean", BF16, nc.sync)
         load_w("u", 0, 0)
         load_w("u", 1, 0)
         load_t(0)
         load_w("u", 2, 0)
         load_w("u", 3, 0)
+        load_t(1)
         load_w("v", 0, 0)
         load_w("v", 1, 0)
         bias_img = load_channels(b_img, "bias_img", BF16, nc.sync)
@@ -296,16 +307,13 @@ def tile_vqa_hadamard_fusion_b15_kernel(
         gain_bf = load_channels(gain, "gain_bf", BF16, nc.sync)
         load_w("u", 0, 1)
         load_w("u", 1, 1)
-        load_t(1)
 
-        widen_x(0, 0, 2, "vector")
-        widen_x(0, 2, 4, "vector")
-        widen_x(1, 0, 2, "scalar")
-        widen_x(1, 2, 4, "vector")
+        for h in range(2):
+            widen_x(h, 0, 1, "vector")
+            widen_x(h, 1, 3, "vector")
+            widen_x(h, 3, 4, "scalar")
         turn_x(0)
         turn_x(1)
-        widen_x(2, 0, 4, "vector")
-        widen_x(3, 0, 4, "vector")
         scale_x(0)
         turn_x(2)
         weave_w("u", 0, 0, "vector")
@@ -314,7 +322,7 @@ def tile_vqa_hadamard_fusion_b15_kernel(
         quant_w("u", 0, 0)
         scale_x(1)
         turn_x(3)
-        turn_t(0, 0)
+        turn_t(0, 0, 0, PACK)
         load_t(2)
         weave_w("u", 1, 0, "vector")
         load_w("u", 2, 1)
@@ -328,35 +336,43 @@ def tile_vqa_hadamard_fusion_b15_kernel(
         weave_x(2)
         quant_w("u", 2, 0)
         scale_x(3)
-        weave_t(0)
+        weave_t(0, 0, PACK)
         weave_w("u", 3, 0, "scalar")
         load_w("v", 0, 1)
         weave_x(3)
         quant_x(2)
-        for c in range(3):
+        for t in range(PACK):
+            a_pass(0, 0, t, 0)
+        turn_t(1, 4, 0, PACK)
+        load_t(3)
+        weave_t(1, 0, PACK)
+        for c in (1, 2):
             for t in range(PACK):
                 a_pass(0, c, t, 0)
-        weave_w("v", 0, 0, "scalar")
+        weave_w("v", 0, 0, "vector")
         quant_x(3)
         quant_w("u", 3, 0)
         for t in range(PACK):
             a_pass(0, 3, t, 0)
-        quant_t(0, 0)
+        quant_t(0)
         weave_w("v", 1, 0, "scalar")
-        quant_t(0, 1)
         quant_w("v", 0, 0)
+        for t in range(PACK):
+            h_pass(0, t, 0)
         weave_w("u", 0, 1, "vector")
         quant_w("v", 1, 0)
         for t in range(PACK):
             a_out(0, t)
         for t in range(PACK):
-            h_mm(0, t)
-        weave_w("u", 1, 1, "vector")
+            h_pass(0, t, 1)
+        quant_t(1)
+        gain_f = sb.tile([P, HALVES, PACK], F32, name="gain_f")
+        nc.scalar.copy(out=gain_f[:], in_=gain_bf[:])
 
         LAST = UNITS - 1
 
         def gains(n):
-            for t in range(PACK):
+            for t in range(1 if n in SCALAR_GAIN else 0, PACK):
                 if t == 2:
                     quant_y(n - 1)
                     if n - 1 == UNITS - 3:
@@ -368,31 +384,25 @@ def tile_vqa_hadamard_fusion_b15_kernel(
             y_out(n, s0 + 1, engine1)
             store_y(n, s0, s0 + 2)
 
-        def quant_t_both(b):
-            for c in range(T_PASSES):
-                quant_t(b, c)
-
-        turn_t(1, 0)
-        load_t(3)
+        turn_t(2, 0, 0, PACK)
         weave_w("u", 3, 1, "scalar")
-        weave_t(1)
+        weave_t(2, 0, PACK)
         for t in range(PACK):
             product(0, t)
+            h_mm(1, t)
         squash(0, 0, 2)
         squash(0, 2, 4)
+        weave_w("u", 1, 1, "vector")
         quant_w("u", 0, 1)
+        quant_w("u", 3, 1)
+        weave_w("u", 2, 1, "vector")
         quant_w("u", 1, 1)
         for t in range(PACK):
             for c in range(2):
                 a_pass(1, c, t, 0)
-        weave_w("u", 2, 1, "vector")
-        quant_w("u", 3, 1)
-        quant_t_both(1)
-        for t in range(PACK):
-            h_mm(1, t)
         weave_w("v", 1, 1, "scalar")
-        quant_w("u", 2, 1)
         weave_w("v", 0, 1, "vector")
+        quant_w("u", 2, 1)
         for t in range(PACK):
             for c in range(2, X_PASSES):
                 a_pass(1, c, t, 0)
@@ -418,41 +428,49 @@ def tile_vqa_hadamard_fusion_b15_kernel(
 
         for n in range(2, UNITS):
             nxt = n < LAST
-            late = n in (2, 4)
+            late = n == T3_AT
             if nxt:
-                y_pair_out(n - 2, 0, "vector" if late else "scalar", "scalar")
+                y_pair_out(n - 2, 0, "vector" if late and VCOPY else "scalar", "scalar")
                 y_pair_out(n - 2, 2, "scalar", "scalar")
             if late:
-                turn_t(n // 2 + 1, 0)
-                weave_t(n // 2 + 1)
-            if n in (3, 5):
-                quant_t_both((n + 1) // 2)
+                turn_t(3, 0, 0, PACK)
+                weave_t(3, 0, PACK)
+            if n in TQ:
+                quant_t(TQ[n])
             gains(n - 1)
             pool = POOL_TOKENS_LONG if n >= LAST - 1 else POOL_TOKENS
             weave_y(n - 1, 0, pool, "gpsimd")
-            if not late:
+            if not late and not SPREAD:
                 turn_y(n - 1, 0, 2)
             product(n, 0)
             product(n, 1)
+            if nxt:
+                h_mm(n + 1, 0)
+            if not late and SPREAD:
+                turn_y(n - 1, 0, 2)
             if n == LAST:
                 y_pair_out(n - 1, 0, "scalar", "scalar")
             squash(n, 0, 2)
+            product(n, 2)
+            squash(n, 2, 3)
             if nxt:
-                h_mm(n + 1, 0)
                 h_mm(n + 1, 1)
+                if SPREAD:
+                    h_mm(n + 1, 2)
             if late:
                 turn_y(n - 1, 0, 2)
             else:
                 turn_y(n - 1, 2, 4)
-            product(n, 2)
-            squash(n, 2, 3)
             product(n, 3)
             squash(n, 3, 4)
             if nxt:
-                h_mm(n + 1, 2)
+                if not SPREAD:
+                    h_mm(n + 1, 2)
                 h_mm(n + 1, 3)
             if late:
                 turn_y(n - 1, 2, 4)
+            if n in SCALAR_GAIN:
+                nc.scalar.activation(out=z[n][:, 0, :], in_=z[n][:, 0, :], func=ACT.Copy, scale=gain_f[:, UNIT_ORDER[n][0], 0:1])
             if n == LAST - 1:
                 y_pair_out(n - 1, 0, "vector", "vector")
                 y_pair_out(n - 1, 2, "scalar", "scalar")
@@ -468,6 +486,8 @@ def tile_vqa_hadamard_fusion_b15_kernel(
         quant_y(LAST - 1)
         weave_y(LAST, 0, SPAN, "vector")
         y_pair_out(LAST, 0, "scalar", "scalar")
-        y_pair_out(LAST, 2, "scalar", "scalar")
+        for s in (2, 3):
+            y_out(LAST, s, "scalar")
+            store_y(LAST, s, s + 1)
         quant_y(LAST)
         store_scales(GROUPS - 1, GROUPS)

from contextlib import ExitStack

import concourse.mybir as mybir
from concourse.masks import make_identity

B, R, K, C, F = 512, 4, 2048, 1024, 1024
FLOPS = 2 * B * K * F + 2 * B * R * C * F

F32 = mybir.dt.float32
BF16 = mybir.dt.bfloat16
U32 = mybir.dt.uint32
I32 = mybir.dt.int32
U8 = mybir.dt.uint8
FP8 = mybir.dt.float8_e4m3fn
FP8X4 = mybir.dt.float8_e4m3fn_x4
ACT = mybir.ActivationFunctionType
ALU = mybir.AluOpType

P = 128
PACK = 4
SPAN = P * PACK
X_PASSES = K // SPAN
T_PASSES = C // SPAN
HALVES = F // SPAN
GROUPS = B * R // SPAN
UNIT_ORDER = [(0, 0), (0, 1), (1, 0), (1, 1)] + [(g, b) for b in range(2, GROUPS) for g in range(HALVES)]
UNITS = len(UNIT_ORDER)
POOL_TOKENS = 256
POOL_TOKENS_LONG = 448
SCALAR_GAIN = (4, 5)
TQ = {3: 2, 5: 3}
T3_AT = 3
VCOPY = 0
SPREAD = 0


def tile_vqa_hadamard_fusion_b15_kernel(
    tc, X_bytes, X_scale, X_mean, U, T, V, b_img, b_txt, gain, out_0, out_1, out_2
):
    nc = tc.nc
    y_rows = out_0.rearrange("i j f -> (i j) f")
    words_out = out_1.rearrange("g p m t -> g p (m t)").bitcast(I32)
    scales_out = out_2.bitcast(I32)

    with ExitStack() as ctx:
        sb = ctx.enter_context(tc.tile_pool(name="sb", bufs=1))
        psum = ctx.enter_context(tc.psum_pool(name="psum", bufs=1))
        ctx.enter_context(tc.manual_schedule())

        def bank(i):
            return psum.tile([P, SPAN], F32, name="bank%d" % i)

        x_raw, x_wide, x_banks, x_planes, x_woven, x_mx = {}, {}, {}, {}, {}, {}
        w_raw, w_woven, w_mx = {}, {}, {}
        t_raw, t_banks, t_woven, t_mx = {}, {}, {}, {}
        a_banks, h_banks, z, y_banks, y_stage, y_woven = {}, {}, {}, {}, {}, {}

        def quantize(src, tag, bufs):
            codes = sb.tile([P, SPAN], U32, name=tag + "_codes", bufs=bufs, align_bytes=64)
            scales = sb.tile([P, SPAN], U8, name=tag + "_scales", bufs=bufs, align_bytes=64)
            nc.vector.quantize_mx(out=codes[:].bitcast(FP8X4), scales=scales[:], in_=src)
            return codes[:], scales[:]

        def mx_pass(acc, weights, t, moving, first, last):
            cols = slice(P * t, P * (t + 1))
            nc.tensor.matmul_mx(
                out=acc[:],
                lhsT=weights[0][:, cols].bitcast(FP8X4),
                lhsT_scale=weights[1][:, cols],
                rhs=moving[0].bitcast(FP8X4),
                rhs_scale=moving[1],
                start=first,
                stop=last,
            )

        def copy_on(engine, out, in_):
            if engine == "scalar":
                nc.scalar.copy(out=out, in_=in_)
            else:
                nc.vector.tensor_copy(out=out, in_=in_)

        def load_x(h):
            x_raw[h] = sb.tile([P, GROUPS, K // 2], U8, name="x_bytes", bufs=2)
            nc.sync.dma_start(
                out=x_raw[h][:], in_=X_bytes[:, K // 2 * h : K // 2 * (h + 1)].rearrange("(b p) k -> p b k", p=P)
            )

        def load_channels(vec, name, dtype, queue):
            n = vec.shape[1] // SPAN
            vals = sb.tile([P, n, PACK], dtype, name=name)
            queue.dma_start(out=vals[:], in_=vec.rearrange("o (g p t) -> p (o g) t", p=P, t=PACK))
            return vals

        def load_w(which, c, g):
            W = U if which == "u" else V
            raw = sb.tile([P, PACK, SPAN], BF16, name="w_raw", bufs=8)
            w_raw[which, c, g] = raw
            nc.sync.dma_start(
                out=raw[:],
                in_=W[SPAN * c : SPAN * (c + 1), SPAN * g : SPAN * (g + 1)].rearrange("(p j) f -> p j f", j=PACK),
            )

        def load_t(b):
            t_raw[b] = sb.tile([P, PACK, C], BF16, name="t_raw", bufs=2)
            nc.sync.dma_start(
                out=t_raw[b][:], in_=T[SPAN * b : SPAN * (b + 1), :].rearrange("(s p) k -> p s k", p=P)
            )

        def widen_x(h, b0, b1, engine):
            if h not in x_wide:
                x_wide[h] = sb.tile([P, GROUPS * K // 2], BF16, name="x_wide", tag="turned_rows", bufs=2, align_bytes=64)
            src = x_raw[h][:, b0:b1, :].rearrange("p b k -> p (b k)").bitcast(FP8)
            dst = x_wide[h][:, K // 2 * b0 : K // 2 * b1]
            if engine == "scalar":
                nc.scalar.activation(out=dst, in_=src, func=ACT.Copy)
            else:
                nc.vector.tensor_copy(out=dst, in_=src)

        def turn_x(c):
            words = x_wide[c // 2][:].bitcast(F32)
            for u in range(2):
                x_banks[c, u] = bank(4 + 2 * (c % 2) + u)
                for b in range(GROUPS):
                    w0 = 512 * b + 256 * (c % 2)
                    nc.tensor.transpose(x_banks[c, u][:, P * b : P * (b + 1)], words[:, w0 + u : w0 + 256 : 2], ident[:])

        def scale_x(c):
            x_planes[c] = sb.tile([P, PACK, SPAN], BF16, name="x_planes", bufs=3)
            for t in range(PACK):
                u, e = divmod(t, 2)
                nc.scalar.activation(
                    out=x_planes[c][:, t, :],
                    in_=x_banks[c, u][:].bitcast(BF16)[:, e::2],
                    func=ACT.Identity,
                    scale=x_scale[:, c, t : t + 1],
                    bias=x_mean[:, c, t : t + 1],
                )

        def interleave(engine, dst, src):
            copy_on(
                engine,
                dst.rearrange("p (c i t) -> p c t i", i=4, t=PACK),
                src.rearrange("p t (c i) -> p c t i", i=4),
            )

        def weave_x(c):
            x_woven[c] = sb.tile([P, PACK * SPAN], BF16, name="x_woven", tag="woven", bufs=5, align_bytes=64)
            interleave("vector", x_woven[c][:], x_planes[c][:])

        def quant_x(c):
            x_mx[c] = quantize(x_woven[c][:], "x", X_PASSES)

        def weave_w(which, c, g, engine):
            dst = sb.tile([P, PACK * SPAN], BF16, name="w_woven", tag="woven", bufs=5, align_bytes=64)
            w_woven[which, c, g] = dst
            copy_on(
                engine,
                dst[:].rearrange("p (t a l j) -> p a j l t", t=PACK, l=2, j=PACK),
                w_raw[which, c, g][:].rearrange("p j (a l t) -> p a j l t", l=2, t=PACK),
            )

        def quant_w(which, c, g):
            w_mx[which, c, g] = quantize(w_woven[which, c, g][:], which, 4)

        def turn_t(b, bank0, s0, s1):
            words = t_raw[b][:].bitcast(F32)
            for s in range(s0, s1):
                t_banks[b, s] = bank(bank0 + s)
                for c in range(T_PASSES):
                    for u in range(2):
                        o = P * (2 * c + u)
                        nc.tensor.transpose(
                            t_banks[b, s][:, o : o + P], words[:, s, 256 * c + u : 256 * (c + 1) : 2], ident[:]
                        )

        def weave_t(b, s0, s1):
            if b not in t_woven:
                t_woven[b] = sb.tile([P, T_PASSES, PACK * SPAN], BF16, name="t_woven", tag="turned_rows", bufs=2, align_bytes=64)
            words = t_woven[b][:].bitcast(F32)
            for s in range(s0, s1):
                nc.scalar.copy(
                    out=words[:, :, 256 * s : 256 * (s + 1)].rearrange("p c (r u) -> p c r u", u=2),
                    in_=t_banks[b, s][:].rearrange("p (c u r) -> p c r u", c=T_PASSES, u=2),
                )

        def quant_t(b):
            codes = sb.tile([P, T_PASSES * SPAN], U32, name="t_codes", bufs=GROUPS, align_bytes=64)
            scales = sb.tile([P, T_PASSES * SPAN], U8, name="t_scales", bufs=GROUPS, align_bytes=64)
            nc.vector.quantize_mx(
                out=codes[:].bitcast(FP8X4), scales=scales[:], in_=t_woven[b][:].rearrange("p c w -> p (c w)")
            )
            for c in range(T_PASSES):
                cols = slice(SPAN * c, SPAN * (c + 1))
                t_mx[b, c] = codes[:, cols], scales[:, cols]

        def a_pass(g, c, t, bank0):
            if c == 0:
                a_banks[g, t] = bank(bank0 + t)
            mx_pass(a_banks[g, t], w_mx["u", c, g], t, x_mx[c], c == 0, c == X_PASSES - 1)

        def a_out(g, t):
            nc.scalar.activation(
                out=a_sb[:, g, t, :], in_=a_banks[g, t][:], func=ACT.Identity, bias=bias_img[:, g, t : t + 1]
            )

        def h_pass(n, t, c):
            g, b = UNIT_ORDER[n]
            if c == 0:
                h_banks[n, t] = bank(4 + t)
            mx_pass(h_banks[n, t], w_mx["v", c, g], t, t_mx[b, c], c == 0, c == T_PASSES - 1)

        def h_mm(n, t):
            for c in range(T_PASSES):
                h_pass(n, t, c)

        def product(n, t):
            g, b = UNIT_ORDER[n]
            if t == 0:
                z[n] = sb.tile([P, PACK, SPAN], F32, name="z", bufs=3)
            nc.vector.scalar_tensor_tensor(
                out=z[n][:, t, :].rearrange("p (i j) -> p i j", j=R),
                in0=h_banks[n, t][:].rearrange("p (i j) -> p i j", j=R),
                scalar=bias_txt[:, g, t : t + 1],
                in1=a_sb[:, g, t, P * b : P * (b + 1)].unsqueeze(2).to_broadcast([P, P, R]),
                op0=ALU.add,
                op1=ALU.mult,
            )

        def squash(n, t0, t1):
            nc.scalar.activation(out=z[n][:, t0:t1, :], in_=z[n][:, t0:t1, :], func=ACT.Tanh)

        def apply_gain(n, t, m0, m1):
            g = UNIT_ORDER[n][0]
            rows = z[n][:, t, m0:m1]
            nc.vector.tensor_scalar(out=rows, in0=rows, scalar1=gain_bf[:, g, t : t + 1], scalar2=None, op0=ALU.mult)

        def turn_y(n, s0, s1):
            for s in range(s0, s1):
                y_banks[n, s] = bank(s)
                for t in range(PACK):
                    nc.tensor.transpose(y_banks[n, s][:, P * t : P * (t + 1)], z[n][:, t, P * s : P * (s + 1)], ident[:])

        def y_out(n, s, engine):
            if n not in y_stage:
                y_stage[n] = sb.tile([P, PACK, SPAN], F32, name="y_stage", bufs=2)
            copy_on(
                engine,
                y_stage[n][:, s, :].rearrange("m (p t) -> m p t", t=PACK),
                y_banks[n, s][:].rearrange("m (t p) -> m p t", t=PACK),
            )

        def store_y(n, s0, s1):
            g, b = UNIT_ORDER[n]
            rows = y_rows[SPAN * b + P * s0 : SPAN * b + P * s1, SPAN * g : SPAN * (g + 1)]
            nc.sync.dma_start(out=rows.rearrange("(s m) f -> m s f", m=P), in_=y_stage[n][:, s0:s1, :])

        def weave_y(n, m0, m1, engine):
            if n not in y_woven:
                y_woven[n] = sb.tile([P, PACK * SPAN], BF16, name="y_woven", bufs=3, align_bytes=64)
            dst, src = y_woven[n][:, PACK * m0 : PACK * m1], z[n][:, :, m0:m1]
            if engine == "gpsimd":
                nc.gpsimd.tensor_scalar(
                    out=dst.rearrange("p (m t) -> p m t", t=PACK),
                    in0=src.rearrange("p t m -> p m t"),
                    scalar1=1.0,
                    scalar2=1.0,
                    op0=ALU.mult,
                    op1=ALU.mult,
                )
            else:
                interleave(engine, dst, src)

        def quant_y(n):
            g, b = UNIT_ORDER[n]
            codes = sb.tile([P, SPAN], U32, name="y_codes", bufs=3, align_bytes=64)
            nc.vector.quantize_mx(
                out=codes[:].bitcast(FP8X4), scales=y_scales[4 * g :, SPAN * b : SPAN * (b + 1)], in_=y_woven[n][:]
            )
            nc.sync.dma_start(out=words_out[g, :, SPAN * b : SPAN * (b + 1)], in_=codes[:].bitcast(I32))

        def store_scales(b0, b1):
            cols = slice(P * b0, P * b1)
            for q in range(4):
                nc.sync.dma_start(
                    out=scales_out[:, 4 * q : 4 * q + 4, cols], in_=y_scales[32 * q : 32 * q + 8, :].bitcast(I32)[:, cols]
                )

        ident = sb.tile([P, P], F32, name="ident")
        make_identity(nc, ident[:])
        a_sb = sb.tile([P, HALVES, PACK, SPAN], F32, name="a_sb")

        y_scales = sb.tile([P, GROUPS * SPAN], U8, name="y_scales", align_bytes=64)
        load_x(0)
        load_x(1)
        x_scale = load_channels(X_scale, "x_scale", F32, nc.sync)
        x_mean = load_channels(X_mean, "x_mean", BF16, nc.sync)
        load_w("u", 0, 0)
        load_w("u", 1, 0)
        load_t(0)
        load_w("u", 2, 0)
        load_w("u", 3, 0)
        load_t(1)
        load_w("v", 0, 0)
        load_w("v", 1, 0)
        bias_img = load_channels(b_img, "bias_img", BF16, nc.sync)
        bias_txt = load_channels(b_txt, "bias_txt", BF16, nc.sync)
        gain_bf = load_channels(gain, "gain_bf", BF16, nc.sync)
        load_w("u", 0, 1)
        load_w("u", 1, 1)

        for h in range(2):
            widen_x(h, 0, 1, "vector")
            widen_x(h, 1, 3, "vector")
            widen_x(h, 3, 4, "scalar")
        turn_x(0)
        turn_x(1)
        scale_x(0)
        turn_x(2)
        weave_w("u", 0, 0, "vector")
        load_w("u", 3, 1)
        weave_x(0)
        quant_w("u", 0, 0)
        scale_x(1)
        turn_x(3)
        turn_t(0, 0, 0, PACK)
        load_t(2)
        weave_w("u", 1, 0, "vector")
        load_w("u", 2, 1)
        quant_x(0)
        weave_x(1)
        quant_w("u", 1, 0)
        scale_x(2)
        weave_w("u", 2, 0, "vector")
        load_w("v", 1, 1)
        quant_x(1)
        weave_x(2)
        quant_w("u", 2, 0)
        scale_x(3)
        weave_t(0, 0, PACK)
        weave_w("u", 3, 0, "scalar")
        load_w("v", 0, 1)
        weave_x(3)
        quant_x(2)
        for t in range(PACK):
            a_pass(0, 0, t, 0)
        turn_t(1, 4, 0, PACK)
        load_t(3)
        weave_t(1, 0, PACK)
        for c in (1, 2):
            for t in range(PACK):
                a_pass(0, c, t, 0)
        weave_w("v", 0, 0, "vector")
        quant_x(3)
        quant_w("u", 3, 0)
        for t in range(PACK):
            a_pass(0, 3, t, 0)
        quant_t(0)
        weave_w("v", 1, 0, "scalar")
        quant_w("v", 0, 0)
        for t in range(PACK):
            h_pass(0, t, 0)
        weave_w("u", 0, 1, "vector")
        quant_w("v", 1, 0)
        for t in range(PACK):
            a_out(0, t)
        for t in range(PACK):
            h_pass(0, t, 1)
        quant_t(1)
        gain_f = sb.tile([P, HALVES, PACK], F32, name="gain_f")
        nc.scalar.copy(out=gain_f[:], in_=gain_bf[:])

        LAST = UNITS - 1

        def gains(n):
            for t in range(1 if n in SCALAR_GAIN else 0, PACK):
                if t == 2:
                    quant_y(n - 1)
                    if n - 1 == UNITS - 3:
                        store_scales(0, GROUPS - 1)
                apply_gain(n, t, 0, SPAN)

        def y_pair_out(n, s0, engine0, engine1):
            y_out(n, s0, engine0)
            y_out(n, s0 + 1, engine1)
            store_y(n, s0, s0 + 2)

        turn_t(2, 0, 0, PACK)
        weave_w("u", 3, 1, "scalar")
        weave_t(2, 0, PACK)
        for t in range(PACK):
            product(0, t)
            h_mm(1, t)
        squash(0, 0, 2)
        squash(0, 2, 4)
        weave_w("u", 1, 1, "vector")
        quant_w("u", 0, 1)
        quant_w("u", 3, 1)
        weave_w("u", 2, 1, "vector")
        quant_w("u", 1, 1)
        for t in range(PACK):
            for c in range(2):
                a_pass(1, c, t, 0)
        weave_w("v", 1, 1, "scalar")
        weave_w("v", 0, 1, "vector")
        quant_w("u", 2, 1)
        for t in range(PACK):
            for c in range(2, X_PASSES):
                a_pass(1, c, t, 0)
            a_out(1, t)

        apply_gain(0, 0, 0, SPAN)
        apply_gain(0, 1, 0, SPAN)
        quant_w("v", 0, 1)
        apply_gain(0, 2, 0, SPAN)
        apply_gain(0, 3, 0, SPAN)
        weave_y(0, 0, POOL_TOKENS, "gpsimd")
        for t in range(PACK):
            product(1, t)
            h_pass(2, t, 0)
        squash(1, 0, 2)
        squash(1, 2, 4)
        turn_y(0, 0, 2)
        quant_w("v", 1, 1)
        weave_y(0, POOL_TOKENS, SPAN, "vector")
        for t in range(PACK):
            h_pass(2, t, 1)
        turn_y(0, 2, PACK)

        for n in range(2, UNITS):
            nxt = n < LAST
            late = n == T3_AT
            if nxt:
                y_pair_out(n - 2, 0, "vector" if late and VCOPY else "scalar", "scalar")
                y_pair_out(n - 2, 2, "scalar", "scalar")
            if late:
                turn_t(3, 0, 0, PACK)
                weave_t(3, 0, PACK)
            if n in TQ:
                quant_t(TQ[n])
            gains(n - 1)
            pool = POOL_TOKENS_LONG if n >= LAST - 1 else POOL_TOKENS
            weave_y(n - 1, 0, pool, "gpsimd")
            if not late and not SPREAD:
                turn_y(n - 1, 0, 2)
            product(n, 0)
            product(n, 1)
            if nxt:
                h_mm(n + 1, 0)
            if not late and SPREAD:
                turn_y(n - 1, 0, 2)
            if n == LAST:
                y_pair_out(n - 1, 0, "scalar", "scalar")
            squash(n, 0, 2)
            product(n, 2)
            squash(n, 2, 3)
            if nxt:
                h_mm(n + 1, 1)
                if SPREAD:
                    h_mm(n + 1, 2)
            if late:
                turn_y(n - 1, 0, 2)
            else:
                turn_y(n - 1, 2, 4)
            product(n, 3)
            squash(n, 3, 4)
            if nxt:
                if not SPREAD:
                    h_mm(n + 1, 2)
                h_mm(n + 1, 3)
            if late:
                turn_y(n - 1, 2, 4)
            if n in SCALAR_GAIN:
                nc.scalar.activation(out=z[n][:, 0, :], in_=z[n][:, 0, :], func=ACT.Copy, scale=gain_f[:, UNIT_ORDER[n][0], 0:1])
            if n == LAST - 1:
                y_pair_out(n - 1, 0, "vector", "vector")
                y_pair_out(n - 1, 2, "scalar", "scalar")
            elif n == LAST:
                y_pair_out(n - 1, 2, "vector", "vector")
            weave_y(n - 1, pool, SPAN, "vector")
        for t in range(PACK):
            apply_gain(LAST, t, 0, SPAN // 2)
        turn_y(LAST, 0, 2)
        for t in range(PACK):
            apply_gain(LAST, t, SPAN // 2, SPAN)
        turn_y(LAST, 2, PACK)
        quant_y(LAST - 1)
        weave_y(LAST, 0, SPAN, "vector")
        y_pair_out(LAST, 0, "scalar", "scalar")
        for s in (2, 3):
            y_out(LAST, s, "scalar")
            store_y(LAST, s, s + 1)
        quant_y(LAST)
        store_scales(GROUPS - 1, GROUPS)
